import numpy as np
import ml_dtypes


def mxq(x, axis, fmt="e4m3"):
    dtype, down = {"e4m3": (ml_dtypes.float8_e4m3fn, 7), "e5m2": (ml_dtypes.float8_e5m2, 14)}[fmt]
    v = np.moveaxis(np.asarray(x, np.float32).astype(ml_dtypes.bfloat16).astype(np.float64), axis, -1)
    blocks = v.reshape(v.shape[:-1] + (-1, 32))
    amax = np.abs(blocks).max(-1, keepdims=True)
    byte = np.maximum(np.where(amax > 0, np.frexp(amax)[1] - 1 + 127, 0) - down, 1)
    scale = np.exp2(byte - 127.0)
    codes = (blocks / scale).astype(np.float32).astype(dtype).astype(np.float64)
    return np.moveaxis((codes * scale).reshape(v.shape), -1, axis)


WIDE = False


def mx_kscale(k):
    if not WIDE:
        return np.ones(k)
    levels = np.array([10, -10, 5, -5, 0])
    if k % 512:
        return np.exp2(np.random.permutation(np.resize(levels, k // 32))).repeat(32)
    a = np.empty((k // 512, 16))
    for p in range(k // 512):
        a[p, :8] = np.random.permutation(np.resize(levels, 8))
        for g in range(8):
            far = levels[np.abs(levels - a[p, g]) >= 10]
            a[p, g + 8] = far[np.random.randint(len(far))]
    return np.exp2(a.ravel()).repeat(32)


def f64(x):
    return np.asarray(x).astype(np.float64)


E2M1 = np.array([0.0, 0.5, 1.0, 1.5, 2.0, 3.0, 4.0, 6.0, -0.0, -0.5, -1.0, -1.5, -2.0, -3.0, -4.0, -6.0])


def pack_weight(w, fmt):
    k, n = w.shape
    w = f64(np.asarray(w, np.float32).astype(ml_dtypes.bfloat16)).reshape(k // 32, 32, n)
    amax = np.abs(w).max(1)
    if fmt == "e4m3":
        byte = np.frexp(amax)[1] - 1 + 127 - 7
    else:
        mant, ex = np.frexp(amax / 6.0)
        byte = np.where(mant > 0.5, ex, ex - 1) + 127
    byte = np.clip(np.where(amax > 0, byte, 1), 1, 254)
    scaled = (w * np.exp2(127.0 - byte)[:, None, :]).reshape(k, n).astype(np.float32)
    by_word = np.ascontiguousarray(scaled.reshape(k // 512, 128, 4, n).transpose(0, 1, 3, 2))
    if fmt == "e4m3":
        words = by_word.astype(ml_dtypes.float8_e4m3fn).view(np.uint8)
    else:
        c = by_word.astype(ml_dtypes.float4_e2m1fn).view(np.uint8) & 0xF
        words = (c[..., 0::2] | (c[..., 1::2] << 4)).reshape(k // 512, 128, 2 * n)
    return np.ascontiguousarray(words), np.ascontiguousarray(byte.astype(np.uint8).reshape(k // 512, 16, n))


def unpack_weight(words, scales, fmt):
    g, _, n = scales.shape
    words = np.ascontiguousarray(words).reshape(g, 128, n, -1)
    if fmt == "e4m3":
        vals = words.view(ml_dtypes.float8_e4m3fn).astype(np.float64)
    else:
        nib = np.empty((g, 128, n, 4), np.uint8)
        nib[..., 0::2] = words & 0xF
        nib[..., 1::2] = words >> 4
        vals = E2M1[nib]
    vals = vals * np.repeat(np.exp2(scales.astype(np.float64) - 127.0), 8, axis=1)[..., None]
    return vals.transpose(0, 1, 3, 2).reshape(g * 512, n)


D, K, M, T = 256, 1024, 1536, 1024


def setup_inputs():
    n = np.random.standard_normal
    s = mx_kscale(K)[:, None]
    p_w0 = pack_weight(n((K, M)) / np.sqrt(K) / s, "e2m1")
    p_w1 = pack_weight(n((K, M)) / np.sqrt(K) / s, "e4m3")
    return {
        "x": (n((K, T + 2 * D)) * s).astype(np.float32),
        "w0_words": p_w0[0],
        "w0_scales": p_w0[1],
        "w1_words": p_w1[0],
        "w1_scales": p_w1[1],
        "w2": (n((K, M)) / np.sqrt(K) / s).astype(np.float32),
        "g": (n((1024, 1536))).astype(np.float32),
    }


def reference(x, w0_words, w0_scales, w1_words, w1_scales, w2, g):
    x_ = mxq(f64(x), 0, "e4m3")
    w0_ = unpack_weight(w0_words, w0_scales, "e2m1")
    w1_ = unpack_weight(w1_words, w1_scales, "e4m3")
    w2_ = mxq(f64(w2), 0, "e4m3")
    y = x_[:, :T].T @ w0_ + x_[:, D:D + T].T @ w1_ + x_[:, 2 * D:].T @ w2_
    return f64(g) * y

@@ -1,0 +1,218 @@
+from contextlib import ExitStack
+
+import concourse.mybir as mybir
+
+D, K, M, T = 256, 1024, 1536, 1024
+FLOPS = 2 * 3 * K * M * T
+
+F32 = mybir.dt.float32
+BF16 = mybir.dt.bfloat16
+I32 = mybir.dt.int32
+U32 = mybir.dt.uint32
+U8 = mybir.dt.uint8
+FP8X4 = mybir.dt.float8_e4m3fn_x4
+FP4X4 = mybir.dt.float4_e2m1fn_x4
+MULT = mybir.AluOpType.mult
+
+P = 128
+PACK = 4
+K_PASS = P * PACK
+PASSES = K // K_PASS
+N = 512
+XW = T + 2 * D
+T_TILES = T // P
+W1_ROW = 4
+SCALAR_COLS = 256
+
+
+def tile_mix_dconv_tm_mul_kernel(tc, x, w0_words, w0_scales, w1_words, w1_scales, w2, g, out):
+    nc = tc.nc
+    with ExitStack() as ctx:
+        keep = ctx.enter_context(tc.tile_pool(name="keep", bufs=1))
+        stage = ctx.enter_context(tc.tile_pool(name="stage", bufs=4))
+        psum = ctx.enter_context(tc.psum_pool(name="psum", bufs=1))
+        ctx.enter_context(tc.manual_schedule())
+
+        def kept(name, shape, dtype):
+            return keep.tile(shape, dtype, name=name, align_bytes=64)
+
+        spans = [(0, N), (N, M)]
+        x_raw = [kept("x_raw%d" % a, [P, PACK, XW], F32) for a in range(PASSES)]
+        w2_raw = [[kept("w2_raw%d%d" % (s, a), [P, PACK, hi - lo], F32) for a in range(PASSES)] for s, (lo, hi) in enumerate(spans)]
+        w0_codes = [kept("w0_codes%d" % s, [P, PASSES, 2 * (hi - lo)], U8) for s, (lo, hi) in enumerate(spans)]
+        w1_codes = [kept("w1_codes%d" % s, [P, PASSES, hi - lo], U32) for s, (lo, hi) in enumerate(spans)]
+        w01_plane = kept("w01_plane", [P, PASSES, M], U8)
+        x_codes = [[kept("x_codes%d%d" % (a, c), [P, N], U32) for c in range(XW // N)] for a in range(PASSES)]
+        x_plane = [[kept("x_plane%d%d" % (a, c), [P, N], U8) for c in range(XW // N)] for a in range(PASSES)]
+        w2_codes = [[kept("w2_codes%d%d" % (a, j), [P, N], U32) for j in range(M // N)] for a in range(PASSES)]
+        w2_plane = [[kept("w2_plane%d%d" % (a, j), [P, N], U8) for j in range(M // N)] for a in range(PASSES)]
+        gate = [kept("gate%d" % b, [P, 2, M], F32) for b in range(T_TILES // 2)]
+        parked = [kept("parked%d" % i, [P, N], F32) for i in range(T_TILES)]
+
+        nc.vector.memset(w01_plane[:].rearrange("p a n -> p (a n)").bitcast(I32), 0)
+        for row0, scales in ((0, w0_scales), (W1_ROW, w1_scales)):
+            for r in range(4):
+                nc.sync.dma_start(
+                    out=w01_plane[row0 + r : P : 32].bitcast(I32),
+                    in_=scales.bitcast(I32)[:, r:16:4, :].rearrange("a q n -> q a n"),
+                )
+
+        def load_x(a):
+            rows = x[a * K_PASS : (a + 1) * K_PASS, :]
+            nc.sync.dma_start(out=x_raw[a][:].rearrange("p j w -> p (j w)"), in_=rows.rearrange("(p j) w -> p (j w)", j=PACK))
+
+        def load_w2(s, a):
+            lo, hi = spans[s]
+            rows = w2[a * K_PASS : (a + 1) * K_PASS, lo:hi]
+            nc.sync.dma_start(out=w2_raw[s][a][:], in_=rows.rearrange("(p j) n -> p j n", j=PACK))
+
+        def load_w01(s):
+            lo, hi = spans[s]
+            nc.sync.dma_start(
+                out=w0_codes[s][:].bitcast(I32),
+                in_=w0_words.rearrange("a p n -> p a n")[:, :, 2 * lo : 2 * hi].bitcast(I32),
+            )
+            nc.sync.dma_start(
+                out=w1_codes[s][:].bitcast(I32),
+                in_=w1_words.rearrange("a p n i -> p a (n i)")[:, :, 4 * lo : 4 * hi].bitcast(I32),
+            )
+
+        load_x(0)
+        load_w01(0)
+        load_w2(0, 0)
+        load_x(1)
+        load_w2(0, 1)
+        load_w01(1)
+        load_w2(1, 0)
+        load_w2(1, 1)
+        for b in range(T_TILES // 2):
+            nc.sync.dma_start(out=gate[b][:], in_=g[2 * b * P : 2 * (b + 1) * P, :].rearrange("(e p) n -> p e n", e=2))
+
+        def interleave(raw, col0):
+            grouped = stage.tile([P, N, PACK], BF16, name="grouped", align_bytes=64)
+            for lo, hi, copy in ((0, SCALAR_COLS, nc.scalar.copy), (SCALAR_COLS, N, nc.vector.tensor_copy)):
+                copy(
+                    out=grouped[:, lo:hi, :].rearrange("p (c i) j -> p c j i", i=4),
+                    in_=raw[:, :, col0 + lo : col0 + hi].rearrange("p j (c i) -> p c j i", i=4),
+                )
+            return grouped
+
+        def quantise(chunks):
+            waiting = None
+            for raw, col0, codes, plane in chunks:
+                grouped = interleave(raw, col0)
+                if waiting is not None:
+                    nc.vector.quantize_mx(out=waiting[1][:].bitcast(FP8X4), scales=waiting[2][:], in_=waiting[0][:].rearrange("p n j -> p (n j)"))
+                waiting = (grouped, codes, plane)
+            nc.vector.quantize_mx(out=waiting[1][:].bitcast(FP8X4), scales=waiting[2][:], in_=waiting[0][:].rearrange("p n j -> p (n j)"))
+
+        def x_chunk(a, c):
+            return (x_raw[a], c * N, x_codes[a][c], x_plane[a][c])
+
+        def w2_chunk(a, j):
+            s = min(j, 1)
+            return (w2_raw[s][a], j * N - spans[s][0], w2_codes[a][j], w2_plane[a][j])
+
+        done = {}
+        acc = {}
+
+        def open_group(i, j, bank):
+            acc[i, j] = psum.tile([P, N], F32, name="acc", tag="bank%d" % bank)
+            done[i, j] = 0
+
+        def mm(i, j, tap, a):
+            c, t0 = divmod(i * P + tap * D, N)
+            s = min(j, 1)
+            n0 = j * N - spans[s][0]
+            if tap == 0:
+                rhs = w0_codes[s][:, a, 2 * n0 : 2 * (n0 + N)].bitcast(FP4X4)
+                rhs_scale = w01_plane[:, a, j * N : (j + 1) * N]
+            elif tap == 1:
+                rhs = w1_codes[s][:, a, n0 : n0 + N].bitcast(FP8X4)
+                rhs_scale = w01_plane[W1_ROW:P, a, j * N : (j + 1) * N]
+            else:
+                rhs = w2_codes[a][j][:].bitcast(FP8X4)
+                rhs_scale = w2_plane[a][j][:]
+            nc.tensor.matmul_mx(
+                out=acc[i, j][:],
+                lhsT=x_codes[a][c][:, t0 : t0 + P].bitcast(FP8X4),
+                lhsT_scale=x_plane[a][c][:, t0 : t0 + P],
+                rhs=rhs,
+                rhs_scale=rhs_scale,
+                start=(done[i, j] == 0),
+                stop=(done[i, j] == 3 * PASSES - 1),
+            )
+            done[i, j] += 1
+
+        def first_sweep(a):
+            arrival = {"x0": 0, "x1": 1, "w2": 2, "x2": 3}
+            work = []
+            for i in range(T_TILES):
+                for tap in range(3):
+                    ready = arrival["x%d" % ((i * P + tap * D) // N)]
+                    if tap == 2:
+                        ready = max(ready, arrival["w2"])
+                    work.append((ready, i, tap))
+            for ready, i, tap in sorted(work):
+                mm(i, 0, tap, a)
+
+        def gate_cols(i, j):
+            return gate[i // 2][:, i % 2, j * N : (j + 1) * N]
+
+        def finish(i, j):
+            nc.vector.tensor_tensor(out=gate_cols(i, j), in0=acc[i, j][:], in1=gate_cols(i, j), op=MULT)
+
+        def finish_parked(i):
+            nc.vector.tensor_tensor(out=gate_cols(i, 0), in0=parked[i][:], in1=gate_cols(i, 0), op=MULT)
+
+        def store(i0, i1):
+            b = i0 // 2
+            nc.sync.dma_start(
+                out=out[i0 * P : i1 * P, :].rearrange("(e p) n -> p e n", p=P),
+                in_=gate[b][:, i0 - 2 * b : i1 - 2 * b, :],
+            )
+
+        for i in range(T_TILES):
+            open_group(i, 0, i)
+        for a in range(PASSES):
+            quantise([x_chunk(a, 0), x_chunk(a, 1), w2_chunk(a, 0), x_chunk(a, 2)])
+            first_sweep(a)
+
+        half = T_TILES // 2
+        groups = [(i, j) for i in range(T_TILES) for j in (1, 2)]
+        for bank, (i, j) in enumerate(groups[:T_TILES]):
+            copy = nc.scalar.copy if bank % 2 == 0 else nc.vector.tensor_copy
+            copy(out=parked[bank][:], in_=acc[bank, 0][:])
+            open_group(i, j, bank)
+            for tap in (0, 1):
+                for a in range(PASSES):
+                    mm(i, j, tap, a)
+        quantise([w2_chunk(a, j) for a in range(PASSES) for j in (1, 2)])
+        for j in (1, 2):
+            for i in range(half):
+                mm(i, j, 2, 0)
+        for i, j in groups[:T_TILES]:
+            mm(i, j, 2, 1)
+        for bank, (i, j) in enumerate(groups[:T_TILES]):
+            finish(i, j)
+            if bank % 4 == 3:
+                finish_parked(i - 1)
+                finish_parked(i)
+                store(i - 1, i + 1)
+            i2, j2 = groups[T_TILES + bank]
+            open_group(i2, j2, bank)
+            for tap in range(3):
+                for a in range(PASSES):
+                    mm(i2, j2, tap, a)
+        for i in (4, 5):
+            finish(i, 1)
+            finish(i, 2)
+        finish_parked(4)
+        finish_parked(5)
+        store(4, 6)
+        finish_parked(6)
+        finish_parked(7)
+        for i in (6, 7):
+            finish(i, 1)
+            finish(i, 2)
+            store(i, i + 1)

@@ -52,7 +52,7 @@ def tile_mix_dconv_tm_mul_kernel(tc, x, w0_words, w0_scales, w1_words, w1_scales
         nc.vector.memset(w01_plane[:].rearrange("p a n -> p (a n)").bitcast(I32), 0)
         for row0, scales in ((0, w0_scales), (W1_ROW, w1_scales)):
             for r in range(4):
-                nc.sync.dma_start(
+                nc.gpsimd.dma_start(
                     out=w01_plane[row0 + r : P : 32].bitcast(I32),
                     in_=scales.bitcast(I32)[:, r:16:4, :].rearrange("a q n -> q a n"),
                 )
@@ -212,7 +212,10 @@ def tile_mix_dconv_tm_mul_kernel(tc, x, w0_words, w0_scales, w1_words, w1_scales
         store(4, 6)
         finish_parked(6)
         finish_parked(7)
-        for i in (6, 7):
-            finish(i, 1)
-            finish(i, 2)
-            store(i, i + 1)
+        finish(6, 1)
+        finish(6, 2)
+        store(6, 7)
+        finish(7, 1)
+        nc.sync.dma_start(out=out[7 * P :, : 2 * N], in_=gate[3][:, 1, : 2 * N])
+        finish(7, 2)
+        nc.sync.dma_start(out=out[7 * P :, 2 * N :], in_=gate[3][:, 1, 2 * N :])

@@ -22,7 +22,6 @@ N = 512
 XW = T + 2 * D
 T_TILES = T // P
 W1_ROW = 4
-SCALAR_COLS = 256
 
 
 def tile_mix_dconv_tm_mul_kernel(tc, x, w0_words, w0_scales, w1_words, w1_scales, w2, g, out):
@@ -50,12 +49,14 @@ def tile_mix_dconv_tm_mul_kernel(tc, x, w0_words, w0_scales, w1_words, w1_scales
         parked = [kept("parked%d" % i, [P, N], F32) for i in range(T_TILES)]
 
         nc.vector.memset(w01_plane[:].rearrange("p a n -> p (a n)").bitcast(I32), 0)
-        for row0, scales in ((0, w0_scales), (W1_ROW, w1_scales)):
-            for r in range(4):
-                nc.gpsimd.dma_start(
-                    out=w01_plane[row0 + r : P : 32].bitcast(I32),
-                    in_=scales.bitcast(I32)[:, r:16:4, :].rearrange("a q n -> q a n"),
-                )
+
+        def load_scales(rows):
+            for r in rows:
+                for row0, scales in ((0, w0_scales), (W1_ROW, w1_scales)):
+                    nc.sync.dma_start(
+                        out=w01_plane[row0 + r : P : 32].bitcast(I32),
+                        in_=scales.bitcast(I32)[:, r:16:4, :].rearrange("a q n -> q a n"),
+                    )
 
         def load_x(a):
             rows = x[a * K_PASS : (a + 1) * K_PASS, :]
@@ -78,40 +79,43 @@ def tile_mix_dconv_tm_mul_kernel(tc, x, w0_words, w0_scales, w1_words, w1_scales
             )
 
         load_x(0)
+        load_scales((0, 1))
         load_w01(0)
         load_w2(0, 0)
+        load_scales((2, 3))
         load_x(1)
         load_w2(0, 1)
         load_w01(1)
         load_w2(1, 0)
         load_w2(1, 1)
         for b in range(T_TILES // 2):
-            nc.sync.dma_start(out=gate[b][:], in_=g[2 * b * P : 2 * (b + 1) * P, :].rearrange("(e p) n -> p e n", e=2))
+            nc.sync.dma_start(out=gate[b][:].rearrange("p e n -> p (e n)"), in_=g[b * D : (b + 1) * D, :].rearrange("(p e) n -> p (e n)", e=2))
 
-        def interleave(raw, col0):
-            grouped = stage.tile([P, N, PACK], BF16, name="grouped", align_bytes=64)
-            for lo, hi, copy in ((0, SCALAR_COLS, nc.scalar.copy), (SCALAR_COLS, N, nc.vector.tensor_copy)):
+        def interleave(halves):
+            grouped = stage.tile([P, 2, N // 2, PACK], BF16, name="grouped", align_bytes=64)
+            for h, copy in enumerate((nc.scalar.copy, nc.vector.tensor_copy)):
                 copy(
-                    out=grouped[:, lo:hi, :].rearrange("p (c i) j -> p c j i", i=4),
-                    in_=raw[:, :, col0 + lo : col0 + hi].rearrange("p j (c i) -> p c j i", i=4),
+                    out=grouped[:, h].rearrange("p (c i) j -> p c j i", i=4),
+                    in_=halves[h].rearrange("p j (c i) -> p c j i", i=4),
                 )
             return grouped
 
         def quantise(chunks):
             waiting = None
-            for raw, col0, codes, plane in chunks:
-                grouped = interleave(raw, col0)
+            for halves, codes, plane in chunks:
+                grouped = interleave(halves)
                 if waiting is not None:
-                    nc.vector.quantize_mx(out=waiting[1][:].bitcast(FP8X4), scales=waiting[2][:], in_=waiting[0][:].rearrange("p n j -> p (n j)"))
+                    nc.vector.quantize_mx(out=waiting[1][:].bitcast(FP8X4), scales=waiting[2][:], in_=waiting[0][:].rearrange("p h n j -> p (h n j)"))
                 waiting = (grouped, codes, plane)
-            nc.vector.quantize_mx(out=waiting[1][:].bitcast(FP8X4), scales=waiting[2][:], in_=waiting[0][:].rearrange("p n j -> p (n j)"))
+            nc.vector.quantize_mx(out=waiting[1][:].bitcast(FP8X4), scales=waiting[2][:], in_=waiting[0][:].rearrange("p h n j -> p (h n j)"))
 
         def x_chunk(a, c):
-            return (x_raw[a], c * N, x_codes[a][c], x_plane[a][c])
+            return ([x_raw[a][:, :, c * N + e : (c + 1) * N : 2] for e in range(2)], x_codes[a][c], x_plane[a][c])
 
         def w2_chunk(a, j):
             s = min(j, 1)
-            return (w2_raw[s][a], j * N - spans[s][0], w2_codes[a][j], w2_plane[a][j])
+            n0 = j * N - spans[s][0]
+            return ([w2_raw[s][a][:, :, n0 + h * N // 2 : n0 + (h + 1) * N // 2] for h in range(2)], w2_codes[a][j], w2_plane[a][j])
 
         done = {}
         acc = {}
@@ -121,7 +125,8 @@ def tile_mix_dconv_tm_mul_kernel(tc, x, w0_words, w0_scales, w1_words, w1_scales
             done[i, j] = 0
 
         def mm(i, j, tap, a):
-            c, t0 = divmod(i * P + tap * D, N)
+            c, upper = divmod(i // 2 + tap, 2)
+            t0 = (i % 2) * (N // 2) + upper * P
             s = min(j, 1)
             n0 = j * N - spans[s][0]
             if tap == 0:
@@ -149,11 +154,13 @@ def tile_mix_dconv_tm_mul_kernel(tc, x, w0_words, w0_scales, w1_words, w1_scales
             work = []
             for i in range(T_TILES):
                 for tap in range(3):
-                    ready = arrival["x%d" % ((i * P + tap * D) // N)]
+                    ready = arrival["x%d" % ((i // 2 + tap) // 2)]
                     if tap == 2:
                         ready = max(ready, arrival["w2"])
-                    work.append((ready, i, tap))
-            for ready, i, tap in sorted(work):
+                    if a == 0 and tap < 2:
+                        ready = 4
+                    work.append((ready, tap, i))
+            for ready, tap, i in sorted(work):
                 mm(i, 0, tap, a)
 
         def gate_cols(i, j):
@@ -165,12 +172,12 @@ def tile_mix_dconv_tm_mul_kernel(tc, x, w0_words, w0_scales, w1_words, w1_scales
         def finish_parked(i):
             nc.vector.tensor_tensor(out=gate_cols(i, 0), in0=parked[i][:], in1=gate_cols(i, 0), op=MULT)
 
-        def store(i0, i1):
-            b = i0 // 2
-            nc.sync.dma_start(
-                out=out[i0 * P : i1 * P, :].rearrange("(e p) n -> p e n", p=P),
-                in_=gate[b][:, i0 - 2 * b : i1 - 2 * b, :],
-            )
+        def store_pair(b):
+            nc.sync.dma_start(out=out[b * D : (b + 1) * D, :].rearrange("(p e) n -> p (e n)", e=2), in_=gate[b][:].rearrange("p e n -> p (e n)"))
+
+        def store_part(i, lo, hi):
+            b, e = divmod(i, 2)
+            nc.sync.dma_start(out=out[b * D : (b + 1) * D, :].rearrange("(p e) n -> p e n", e=2)[:, e, lo:hi], in_=gate[b][:, e, lo:hi])
 
         for i in range(T_TILES):
             open_group(i, 0, i)
@@ -198,7 +205,7 @@ def tile_mix_dconv_tm_mul_kernel(tc, x, w0_words, w0_scales, w1_words, w1_scales
             if bank % 4 == 3:
                 finish_parked(i - 1)
                 finish_parked(i)
-                store(i - 1, i + 1)
+                store_pair(i // 2)
             i2, j2 = groups[T_TILES + bank]
             open_group(i2, j2, bank)
             for tap in range(3):
@@ -209,13 +216,13 @@ def tile_mix_dconv_tm_mul_kernel(tc, x, w0_words, w0_scales, w1_words, w1_scales
             finish(i, 2)
         finish_parked(4)
         finish_parked(5)
-        store(4, 6)
+        store_pair(2)
         finish_parked(6)
         finish_parked(7)
         finish(6, 1)
         finish(6, 2)
-        store(6, 7)
+        store_part(6, 0, M)
         finish(7, 1)
-        nc.sync.dma_start(out=out[7 * P :, : 2 * N], in_=gate[3][:, 1, : 2 * N])
+        store_part(7, 0, 2 * N)
         finish(7, 2)
-        nc.sync.dma_start(out=out[7 * P :, 2 * N :], in_=gate[3][:, 1, 2 * N :])
+        store_part(7, 2 * N, M)

@@ -18,65 +18,71 @@ P = 128
 PACK = 4
 K_PASS = P * PACK
 PASSES = K // K_PASS
+TAPS = 3
 N = 512
-XW = T + 2 * D
-T_TILES = T // P
+HALF = N // 2
+RUN = 4
+X_CHUNKS = (T + 2 * D) // N
+N_TILES = M // N
+STRETCHES = T // D
+T_TILES = 2 * STRETCHES
+BANKS = 8
+QUADRANT = 32
 W1_ROW = 4
+W2_SPANS = ((0, N), (N, M))
+STAGE_BUFS = 4
 
 
 def tile_mix_dconv_tm_mul_kernel(tc, x, w0_words, w0_scales, w1_words, w1_scales, w2, g, out):
     nc = tc.nc
     with ExitStack() as ctx:
         keep = ctx.enter_context(tc.tile_pool(name="keep", bufs=1))
-        stage = ctx.enter_context(tc.tile_pool(name="stage", bufs=4))
+        stage = ctx.enter_context(tc.tile_pool(name="stage", bufs=STAGE_BUFS))
         psum = ctx.enter_context(tc.psum_pool(name="psum", bufs=1))
         ctx.enter_context(tc.manual_schedule())
 
         def kept(name, shape, dtype):
             return keep.tile(shape, dtype, name=name, align_bytes=64)
 
-        spans = [(0, N), (N, M)]
-        x_raw = [kept("x_raw%d" % a, [P, PACK, XW], F32) for a in range(PASSES)]
-        w2_raw = [[kept("w2_raw%d%d" % (s, a), [P, PACK, hi - lo], F32) for a in range(PASSES)] for s, (lo, hi) in enumerate(spans)]
-        w0_codes = [kept("w0_codes%d" % s, [P, PASSES, 2 * (hi - lo)], U8) for s, (lo, hi) in enumerate(spans)]
-        w1_codes = [kept("w1_codes%d" % s, [P, PASSES, hi - lo], U32) for s, (lo, hi) in enumerate(spans)]
-        w01_plane = kept("w01_plane", [P, PASSES, M], U8)
-        x_codes = [[kept("x_codes%d%d" % (a, c), [P, N], U32) for c in range(XW // N)] for a in range(PASSES)]
-        x_plane = [[kept("x_plane%d%d" % (a, c), [P, N], U8) for c in range(XW // N)] for a in range(PASSES)]
-        w2_codes = [[kept("w2_codes%d%d" % (a, j), [P, N], U32) for j in range(M // N)] for a in range(PASSES)]
-        w2_plane = [[kept("w2_plane%d%d" % (a, j), [P, N], U8) for j in range(M // N)] for a in range(PASSES)]
-        gate = [kept("gate%d" % b, [P, 2, M], F32) for b in range(T_TILES // 2)]
+        x_raw = [kept("x_raw%d" % a, [P, PACK, T + 2 * D], F32) for a in range(PASSES)]
+        w2_raw = [
+            [kept("w2_raw%d%d" % (s, a), [P, PACK, hi - lo], F32) for a in range(PASSES)]
+            for s, (lo, hi) in enumerate(W2_SPANS)
+        ]
+        w0_codes = [kept("w0_codes%d" % a, [P, 2 * M], U8) for a in range(PASSES)]
+        w1_codes = [kept("w1_codes%d" % a, [P, M], U32) for a in range(PASSES)]
+        w01_planes = kept("w01_planes", [P, PASSES, M], U8)
+        x_codes = [[kept("x_codes%d%d" % (a, c), [P, N], U32) for c in range(X_CHUNKS)] for a in range(PASSES)]
+        x_plane = [[kept("x_plane%d%d" % (a, c), [P, N], U8) for c in range(X_CHUNKS)] for a in range(PASSES)]
+        w2_codes = [[kept("w2_codes%d%d" % (a, j), [P, N], U32) for j in range(N_TILES)] for a in range(PASSES)]
+        w2_plane = [[kept("w2_plane%d%d" % (a, j), [P, N], U8) for j in range(N_TILES)] for a in range(PASSES)]
+        gate = [kept("gate%d" % b, [P, 2, M], F32) for b in range(STRETCHES)]
         parked = [kept("parked%d" % i, [P, N], F32) for i in range(T_TILES)]
 
-        nc.vector.memset(w01_plane[:].rearrange("p a n -> p (a n)").bitcast(I32), 0)
+        nc.vector.memset(w01_planes[:].rearrange("p a n -> p (a n)").bitcast(I32), 0)
 
         def load_scales(rows):
             for r in rows:
                 for row0, scales in ((0, w0_scales), (W1_ROW, w1_scales)):
                     nc.sync.dma_start(
-                        out=w01_plane[row0 + r : P : 32].bitcast(I32),
+                        out=w01_planes[row0 + r : P : QUADRANT].bitcast(I32),
                         in_=scales.bitcast(I32)[:, r:16:4, :].rearrange("a q n -> q a n"),
                     )
 
         def load_x(a):
             rows = x[a * K_PASS : (a + 1) * K_PASS, :]
-            nc.sync.dma_start(out=x_raw[a][:].rearrange("p j w -> p (j w)"), in_=rows.rearrange("(p j) w -> p (j w)", j=PACK))
+            nc.sync.dma_start(
+                out=x_raw[a][:].rearrange("p j w -> p (j w)"), in_=rows.rearrange("(p j) w -> p (j w)", j=PACK)
+            )
 
         def load_w2(s, a):
-            lo, hi = spans[s]
+            lo, hi = W2_SPANS[s]
             rows = w2[a * K_PASS : (a + 1) * K_PASS, lo:hi]
             nc.sync.dma_start(out=w2_raw[s][a][:], in_=rows.rearrange("(p j) n -> p j n", j=PACK))
 
-        def load_w01(s):
-            lo, hi = spans[s]
-            nc.sync.dma_start(
-                out=w0_codes[s][:].bitcast(I32),
-                in_=w0_words.rearrange("a p n -> p a n")[:, :, 2 * lo : 2 * hi].bitcast(I32),
-            )
-            nc.sync.dma_start(
-                out=w1_codes[s][:].bitcast(I32),
-                in_=w1_words.rearrange("a p n i -> p a (n i)")[:, :, 4 * lo : 4 * hi].bitcast(I32),
-            )
+        def load_w01(a):
+            nc.sync.dma_start(out=w0_codes[a][:].bitcast(I32), in_=w0_words[a].bitcast(I32))
+            nc.sync.dma_start(out=w1_codes[a][:].bitcast(I32), in_=w1_words[a].rearrange("p n i -> p (n i)").bitcast(I32))
 
         load_x(0)
         load_scales((0, 1))
@@ -84,145 +90,144 @@ def tile_mix_dconv_tm_mul_kernel(tc, x, w0_words, w0_scales, w1_words, w1_scales
         load_w2(0, 0)
         load_scales((2, 3))
         load_x(1)
-        load_w2(0, 1)
         load_w01(1)
+        load_w2(0, 1)
         load_w2(1, 0)
         load_w2(1, 1)
-        for b in range(T_TILES // 2):
-            nc.sync.dma_start(out=gate[b][:].rearrange("p e n -> p (e n)"), in_=g[b * D : (b + 1) * D, :].rearrange("(p e) n -> p (e n)", e=2))
+        for b in range(STRETCHES):
+            nc.sync.dma_start(
+                out=gate[b][:].rearrange("p e n -> p (e n)"),
+                in_=g[b * D : (b + 1) * D, :].rearrange("(p e) n -> p (e n)", e=2),
+            )
 
-        def interleave(halves):
-            grouped = stage.tile([P, 2, N // 2, PACK], BF16, name="grouped", align_bytes=64)
+        def lay_out(halves):
+            grouped = stage.tile([P, 2, HALF, PACK], BF16, name="grouped", align_bytes=64)
             for h, copy in enumerate((nc.scalar.copy, nc.vector.tensor_copy)):
                 copy(
-                    out=grouped[:, h].rearrange("p (c i) j -> p c j i", i=4),
-                    in_=halves[h].rearrange("p j (c i) -> p c j i", i=4),
+                    out=grouped[:, h].rearrange("p (c i) j -> p c j i", i=RUN),
+                    in_=halves[h].rearrange("p j (c i) -> p c j i", i=RUN),
                 )
             return grouped
+
+        def quantise_one(grouped, codes, plane):
+            nc.vector.quantize_mx(
+                out=codes[:].bitcast(FP8X4), scales=plane[:], in_=grouped[:].rearrange("p h n j -> p (h n j)")
+            )
 
         def quantise(chunks):
             waiting = None
             for halves, codes, plane in chunks:
-                grouped = interleave(halves)
+                grouped = lay_out(halves)
                 if waiting is not None:
-                    nc.vector.quantize_mx(out=waiting[1][:].bitcast(FP8X4), scales=waiting[2][:], in_=waiting[0][:].rearrange("p h n j -> p (h n j)"))
+                    quantise_one(*waiting)
                 waiting = (grouped, codes, plane)
-            nc.vector.quantize_mx(out=waiting[1][:].bitcast(FP8X4), scales=waiting[2][:], in_=waiting[0][:].rearrange("p h n j -> p (h n j)"))
+            quantise_one(*waiting)
 
         def x_chunk(a, c):
             return ([x_raw[a][:, :, c * N + e : (c + 1) * N : 2] for e in range(2)], x_codes[a][c], x_plane[a][c])
 
         def w2_chunk(a, j):
             s = min(j, 1)
-            n0 = j * N - spans[s][0]
-            return ([w2_raw[s][a][:, :, n0 + h * N // 2 : n0 + (h + 1) * N // 2] for h in range(2)], w2_codes[a][j], w2_plane[a][j])
+            n0 = j * N - W2_SPANS[s][0]
+            halves = [w2_raw[s][a][:, :, n0 + h * HALF : n0 + (h + 1) * HALF] for h in range(2)]
+            return (halves, w2_codes[a][j], w2_plane[a][j])
 
-        done = {}
         acc = {}
+        passes_done = {}
 
-        def open_group(i, j, bank):
+        def open_sum(i, j, bank):
             acc[i, j] = psum.tile([P, N], F32, name="acc", tag="bank%d" % bank)
-            done[i, j] = 0
+            passes_done[i, j] = 0
 
-        def mm(i, j, tap, a):
-            c, upper = divmod(i // 2 + tap, 2)
-            t0 = (i % 2) * (N // 2) + upper * P
-            s = min(j, 1)
-            n0 = j * N - spans[s][0]
+        def add_pass(i, j, tap, a):
+            b, e = divmod(i, 2)
+            c, second = divmod(b + tap, 2)
+            t_cols = slice(e * HALF + second * P, e * HALF + (second + 1) * P)
+            n_cols = slice(j * N, (j + 1) * N)
             if tap == 0:
-                rhs = w0_codes[s][:, a, 2 * n0 : 2 * (n0 + N)].bitcast(FP4X4)
-                rhs_scale = w01_plane[:, a, j * N : (j + 1) * N]
+                rhs = w0_codes[a][:, 2 * j * N : 2 * (j + 1) * N].bitcast(FP4X4)
+                rhs_scale = w01_planes[:, a, n_cols]
             elif tap == 1:
-                rhs = w1_codes[s][:, a, n0 : n0 + N].bitcast(FP8X4)
-                rhs_scale = w01_plane[W1_ROW:P, a, j * N : (j + 1) * N]
+                rhs = w1_codes[a][:, n_cols].bitcast(FP8X4)
+                rhs_scale = w01_planes[W1_ROW:P, a, n_cols]
             else:
                 rhs = w2_codes[a][j][:].bitcast(FP8X4)
                 rhs_scale = w2_plane[a][j][:]
             nc.tensor.matmul_mx(
                 out=acc[i, j][:],
-                lhsT=x_codes[a][c][:, t0 : t0 + P].bitcast(FP8X4),
-                lhsT_scale=x_plane[a][c][:, t0 : t0 + P],
+                lhsT=x_codes[a][c][:, t_cols].bitcast(FP8X4),
+                lhsT_scale=x_plane[a][c][:, t_cols],
                 rhs=rhs,
                 rhs_scale=rhs_scale,
-                start=(done[i, j] == 0),
-                stop=(done[i, j] == 3 * PASSES - 1),
+                start=(passes_done[i, j] == 0),
+                stop=(passes_done[i, j] == TAPS * PASSES - 1),
             )
-            done[i, j] += 1
+            passes_done[i, j] += 1
 
-        def first_sweep(a):
-            arrival = {"x0": 0, "x1": 1, "w2": 2, "x2": 3}
-            work = []
-            for i in range(T_TILES):
-                for tap in range(3):
-                    ready = arrival["x%d" % ((i // 2 + tap) // 2)]
-                    if tap == 2:
-                        ready = max(ready, arrival["w2"])
-                    if a == 0 and tap < 2:
-                        ready = 4
-                    work.append((ready, tap, i))
-            for ready, tap, i in sorted(work):
-                mm(i, 0, tap, a)
+        def multiply_gate(i, j, total):
+            cols = gate[i // 2][:, i % 2, j * N : (j + 1) * N]
+            nc.vector.tensor_tensor(out=cols, in0=total[:], in1=cols, op=MULT)
 
-        def gate_cols(i, j):
-            return gate[i // 2][:, i % 2, j * N : (j + 1) * N]
-
-        def finish(i, j):
-            nc.vector.tensor_tensor(out=gate_cols(i, j), in0=acc[i, j][:], in1=gate_cols(i, j), op=MULT)
-
-        def finish_parked(i):
-            nc.vector.tensor_tensor(out=gate_cols(i, 0), in0=parked[i][:], in1=gate_cols(i, 0), op=MULT)
-
-        def store_pair(b):
-            nc.sync.dma_start(out=out[b * D : (b + 1) * D, :].rearrange("(p e) n -> p (e n)", e=2), in_=gate[b][:].rearrange("p e n -> p (e n)"))
+        def store_stretch(b):
+            nc.sync.dma_start(
+                out=out[b * D : (b + 1) * D, :].rearrange("(p e) n -> p (e n)", e=2),
+                in_=gate[b][:].rearrange("p e n -> p (e n)"),
+            )
 
         def store_part(i, lo, hi):
             b, e = divmod(i, 2)
-            nc.sync.dma_start(out=out[b * D : (b + 1) * D, :].rearrange("(p e) n -> p e n", e=2)[:, e, lo:hi], in_=gate[b][:, e, lo:hi])
+            rows = out[b * D : (b + 1) * D, :].rearrange("(p e) n -> p e n", e=2)
+            nc.sync.dma_start(out=rows[:, e, lo:hi], in_=gate[b][:, e, lo:hi])
 
         for i in range(T_TILES):
-            open_group(i, 0, i)
+            open_sum(i, 0, i)
         for a in range(PASSES):
-            quantise([x_chunk(a, 0), x_chunk(a, 1), w2_chunk(a, 0), x_chunk(a, 2)])
-            first_sweep(a)
+            quantise([x_chunk(a, c) for c in range(X_CHUNKS)] + [w2_chunk(a, 0)])
+            for tap in range(TAPS):
+                for i in range(T_TILES):
+                    add_pass(i, 0, tap, a)
 
-        half = T_TILES // 2
-        groups = [(i, j) for i in range(T_TILES) for j in (1, 2)]
-        for bank, (i, j) in enumerate(groups[:T_TILES]):
+        later = [(i, j) for i in range(T_TILES) for j in range(1, N_TILES)]
+        round_two, round_three = later[:BANKS], later[BANKS:]
+
+        for bank, (i, j) in enumerate(round_two):
             copy = nc.scalar.copy if bank % 2 == 0 else nc.vector.tensor_copy
             copy(out=parked[bank][:], in_=acc[bank, 0][:])
-            open_group(i, j, bank)
+            open_sum(i, j, bank)
             for tap in (0, 1):
                 for a in range(PASSES):
-                    mm(i, j, tap, a)
-        quantise([w2_chunk(a, j) for a in range(PASSES) for j in (1, 2)])
-        for j in (1, 2):
-            for i in range(half):
-                mm(i, j, 2, 0)
-        for i, j in groups[:T_TILES]:
-            mm(i, j, 2, 1)
-        for bank, (i, j) in enumerate(groups[:T_TILES]):
-            finish(i, j)
-            if bank % 4 == 3:
-                finish_parked(i - 1)
-                finish_parked(i)
-                store_pair(i // 2)
-            i2, j2 = groups[T_TILES + bank]
-            open_group(i2, j2, bank)
-            for tap in range(3):
+                    add_pass(i, j, tap, a)
+        quantise([w2_chunk(a, j) for a in range(PASSES) for j in range(1, N_TILES)])
+        for j in range(1, N_TILES):
+            for i in range(T_TILES // 2):
+                add_pass(i, j, 2, 0)
+        for i, j in round_two:
+            add_pass(i, j, 2, 1)
+
+        for bank, (i, j) in enumerate(round_two):
+            multiply_gate(i, j, acc[i, j])
+            if i % 2 == 1 and j == N_TILES - 1:
+                multiply_gate(i - 1, 0, parked[i - 1])
+                multiply_gate(i, 0, parked[i])
+                store_stretch(i // 2)
+            i_new, j_new = round_three[bank]
+            open_sum(i_new, j_new, bank)
+            for tap in range(TAPS):
                 for a in range(PASSES):
-                    mm(i2, j2, tap, a)
-        for i in (4, 5):
-            finish(i, 1)
-            finish(i, 2)
-        finish_parked(4)
-        finish_parked(5)
-        store_pair(2)
-        finish_parked(6)
-        finish_parked(7)
-        finish(6, 1)
-        finish(6, 2)
-        store_part(6, 0, M)
-        finish(7, 1)
-        store_part(7, 0, 2 * N)
-        finish(7, 2)
-        store_part(7, 2 * N, M)
+                    add_pass(i_new, j_new, tap, a)
+
+        last_even, last_odd = T_TILES - 2, T_TILES - 1
+        for i, j in round_three[: BANKS // 2]:
+            multiply_gate(i, j, acc[i, j])
+        for i in range(T_TILES // 2, last_even):
+            multiply_gate(i, 0, parked[i])
+        store_stretch(STRETCHES - 2)
+        for i in (last_even, last_odd):
+            multiply_gate(i, 0, parked[i])
+        for j in range(1, N_TILES):
+            multiply_gate(last_even, j, acc[last_even, j])
+        store_part(last_even, 0, M)
+        multiply_gate(last_odd, 1, acc[last_odd, 1])
+        store_part(last_odd, 0, M - N)
+        multiply_gate(last_odd, 2, acc[last_odd, 2])
+        store_part(last_odd, M - N, M)

from contextlib import ExitStack

import concourse.mybir as mybir

D, K, M, T = 256, 1024, 1536, 1024
FLOPS = 2 * 3 * K * M * T

F32 = mybir.dt.float32
BF16 = mybir.dt.bfloat16
I32 = mybir.dt.int32
U32 = mybir.dt.uint32
U8 = mybir.dt.uint8
FP8X4 = mybir.dt.float8_e4m3fn_x4
FP4X4 = mybir.dt.float4_e2m1fn_x4
MULT = mybir.AluOpType.mult

P = 128
PACK = 4
K_PASS = P * PACK
PASSES = K // K_PASS
TAPS = 3
N = 512
HALF = N // 2
RUN = 4
X_CHUNKS = (T + 2 * D) // N
N_TILES = M // N
STRETCHES = T // D
T_TILES = 2 * STRETCHES
BANKS = 8
QUADRANT = 32
W1_ROW = 4
W2_SPANS = ((0, N), (N, M))
STAGE_BUFS = 4


def tile_mix_dconv_tm_mul_kernel(tc, x, w0_words, w0_scales, w1_words, w1_scales, w2, g, out):
    nc = tc.nc
    with ExitStack() as ctx:
        keep = ctx.enter_context(tc.tile_pool(name="keep", bufs=1))
        stage = ctx.enter_context(tc.tile_pool(name="stage", bufs=STAGE_BUFS))
        psum = ctx.enter_context(tc.psum_pool(name="psum", bufs=1))
        ctx.enter_context(tc.manual_schedule())

        def kept(name, shape, dtype):
            return keep.tile(shape, dtype, name=name, align_bytes=64)

        x_raw = [kept("x_raw%d" % a, [P, PACK, T + 2 * D], F32) for a in range(PASSES)]
        w2_raw = [
            [kept("w2_raw%d%d" % (s, a), [P, PACK, hi - lo], F32) for a in range(PASSES)]
            for s, (lo, hi) in enumerate(W2_SPANS)
        ]
        w0_codes = [kept("w0_codes%d" % a, [P, 2 * M], U8) for a in range(PASSES)]
        w1_codes = [kept("w1_codes%d" % a, [P, M], U32) for a in range(PASSES)]
        w01_planes = kept("w01_planes", [P, PASSES, M], U8)
        x_codes = [[kept("x_codes%d%d" % (a, c), [P, N], U32) for c in range(X_CHUNKS)] for a in range(PASSES)]
        x_plane = [[kept("x_plane%d%d" % (a, c), [P, N], U8) for c in range(X_CHUNKS)] for a in range(PASSES)]
        w2_codes = [[kept("w2_codes%d%d" % (a, j), [P, N], U32) for j in range(N_TILES)] for a in range(PASSES)]
        w2_plane = [[kept("w2_plane%d%d" % (a, j), [P, N], U8) for j in range(N_TILES)] for a in range(PASSES)]
        gate = [kept("gate%d" % b, [P, 2, M], F32) for b in range(STRETCHES)]
        parked = [kept("parked%d" % i, [P, N], F32) for i in range(T_TILES)]

        nc.vector.memset(w01_planes[:].rearrange("p a n -> p (a n)").bitcast(I32), 0)

        def load_scales(rows):
            for r in rows:
                for row0, scales in ((0, w0_scales), (W1_ROW, w1_scales)):
                    nc.sync.dma_start(
                        out=w01_planes[row0 + r : P : QUADRANT].bitcast(I32),
                        in_=scales.bitcast(I32)[:, r:16:4, :].rearrange("a q n -> q a n"),
                    )

        def load_x(a):
            rows = x[a * K_PASS : (a + 1) * K_PASS, :]
            nc.sync.dma_start(
                out=x_raw[a][:].rearrange("p j w -> p (j w)"), in_=rows.rearrange("(p j) w -> p (j w)", j=PACK)
            )

        def load_w2(s, a):
            lo, hi = W2_SPANS[s]
            rows = w2[a * K_PASS : (a + 1) * K_PASS, lo:hi]
            nc.sync.dma_start(out=w2_raw[s][a][:], in_=rows.rearrange("(p j) n -> p j n", j=PACK))

        def load_w01(a):
            nc.sync.dma_start(out=w0_codes[a][:].bitcast(I32), in_=w0_words[a].bitcast(I32))
            nc.sync.dma_start(out=w1_codes[a][:].bitcast(I32), in_=w1_words[a].rearrange("p n i -> p (n i)").bitcast(I32))

        load_x(0)
        load_scales((0, 1))
        load_w01(0)
        load_w2(0, 0)
        load_scales((2, 3))
        load_x(1)
        load_w01(1)
        load_w2(0, 1)
        load_w2(1, 0)
        load_w2(1, 1)
        for b in range(STRETCHES):
            nc.sync.dma_start(
                out=gate[b][:].rearrange("p e n -> p (e n)"),
                in_=g[b * D : (b + 1) * D, :].rearrange("(p e) n -> p (e n)", e=2),
            )

        def lay_out(halves):
            grouped = stage.tile([P, 2, HALF, PACK], BF16, name="grouped", align_bytes=64)
            for h, copy in enumerate((nc.scalar.copy, nc.vector.tensor_copy)):
                copy(
                    out=grouped[:, h].rearrange("p (c i) j -> p c j i", i=RUN),
                    in_=halves[h].rearrange("p j (c i) -> p c j i", i=RUN),
                )
            return grouped

        def quantise_one(grouped, codes, plane):
            nc.vector.quantize_mx(
                out=codes[:].bitcast(FP8X4), scales=plane[:], in_=grouped[:].rearrange("p h n j -> p (h n j)")
            )

        def quantise(chunks):
            waiting = None
            for halves, codes, plane in chunks:
                grouped = lay_out(halves)
                if waiting is not None:
                    quantise_one(*waiting)
                waiting = (grouped, codes, plane)
            quantise_one(*waiting)

        def x_chunk(a, c):
            return ([x_raw[a][:, :, c * N + e : (c + 1) * N : 2] for e in range(2)], x_codes[a][c], x_plane[a][c])

        def w2_chunk(a, j):
            s = min(j, 1)
            n0 = j * N - W2_SPANS[s][0]
            halves = [w2_raw[s][a][:, :, n0 + h * HALF : n0 + (h + 1) * HALF] for h in range(2)]
            return (halves, w2_codes[a][j], w2_plane[a][j])

        acc = {}
        passes_done = {}

        def open_sum(i, j, bank):
            acc[i, j] = psum.tile([P, N], F32, name="acc", tag="bank%d" % bank)
            passes_done[i, j] = 0

        def add_pass(i, j, tap, a):
            b, e = divmod(i, 2)
            c, second = divmod(b + tap, 2)
            t_cols = slice(e * HALF + second * P, e * HALF + (second + 1) * P)
            n_cols = slice(j * N, (j + 1) * N)
            if tap == 0:
                rhs = w0_codes[a][:, 2 * j * N : 2 * (j + 1) * N].bitcast(FP4X4)
                rhs_scale = w01_planes[:, a, n_cols]
            elif tap == 1:
                rhs = w1_codes[a][:, n_cols].bitcast(FP8X4)
                rhs_scale = w01_planes[W1_ROW:P, a, n_cols]
            else:
                rhs = w2_codes[a][j][:].bitcast(FP8X4)
                rhs_scale = w2_plane[a][j][:]
            nc.tensor.matmul_mx(
                out=acc[i, j][:],
                lhsT=x_codes[a][c][:, t_cols].bitcast(FP8X4),
                lhsT_scale=x_plane[a][c][:, t_cols],
                rhs=rhs,
                rhs_scale=rhs_scale,
                start=(passes_done[i, j] == 0),
                stop=(passes_done[i, j] == TAPS * PASSES - 1),
            )
            passes_done[i, j] += 1

        def multiply_gate(i, j, total):
            cols = gate[i // 2][:, i % 2, j * N : (j + 1) * N]
            nc.vector.tensor_tensor(out=cols, in0=total[:], in1=cols, op=MULT)

        def store_stretch(b):
            nc.sync.dma_start(
                out=out[b * D : (b + 1) * D, :].rearrange("(p e) n -> p (e n)", e=2),
                in_=gate[b][:].rearrange("p e n -> p (e n)"),
            )

        def store_part(i, lo, hi):
            b, e = divmod(i, 2)
            rows = out[b * D : (b + 1) * D, :].rearrange("(p e) n -> p e n", e=2)
            nc.sync.dma_start(out=rows[:, e, lo:hi], in_=gate[b][:, e, lo:hi])

        for i in range(T_TILES):
            open_sum(i, 0, i)
        for a in range(PASSES):
            quantise([x_chunk(a, c) for c in range(X_CHUNKS)] + [w2_chunk(a, 0)])
            for tap in range(TAPS):
                for i in range(T_TILES):
                    add_pass(i, 0, tap, a)

        later = [(i, j) for i in range(T_TILES) for j in range(1, N_TILES)]
        round_two, round_three = later[:BANKS], later[BANKS:]

        for bank, (i, j) in enumerate(round_two):
            copy = nc.scalar.copy if bank % 2 == 0 else nc.vector.tensor_copy
            copy(out=parked[bank][:], in_=acc[bank, 0][:])
            open_sum(i, j, bank)
            for tap in (0, 1):
                for a in range(PASSES):
                    add_pass(i, j, tap, a)
        quantise([w2_chunk(a, j) for a in range(PASSES) for j in range(1, N_TILES)])
        for j in range(1, N_TILES):
            for i in range(T_TILES // 2):
                add_pass(i, j, 2, 0)
        for i, j in round_two:
            add_pass(i, j, 2, 1)

        for bank, (i, j) in enumerate(round_two):
            multiply_gate(i, j, acc[i, j])
            if i % 2 == 1 and j == N_TILES - 1:
                multiply_gate(i - 1, 0, parked[i - 1])
                multiply_gate(i, 0, parked[i])
                store_stretch(i // 2)
            i_new, j_new = round_three[bank]
            open_sum(i_new, j_new, bank)
            for tap in range(TAPS):
                for a in range(PASSES):
                    add_pass(i_new, j_new, tap, a)

        last_even, last_odd = T_TILES - 2, T_TILES - 1
        for i, j in round_three[: BANKS // 2]:
            multiply_gate(i, j, acc[i, j])
        for i in range(T_TILES // 2, last_even):
            multiply_gate(i, 0, parked[i])
        store_stretch(STRETCHES - 2)
        for i in (last_even, last_odd):
            multiply_gate(i, 0, parked[i])
        for j in range(1, N_TILES):
            multiply_gate(last_even, j, acc[last_even, j])
        store_part(last_even, 0, M)
        multiply_gate(last_odd, 1, acc[last_odd, 1])
        store_part(last_odd, 0, M - N)
        multiply_gate(last_odd, 2, acc[last_odd, 2])
        store_part(last_odd, M - N, M)
